import numpy as np
import ml_dtypes


def mxq(x, axis, fmt="e4m3"):
    dtype, down = {"e4m3": (ml_dtypes.float8_e4m3fn, 7), "e5m2": (ml_dtypes.float8_e5m2, 14)}[fmt]
    v = np.moveaxis(np.asarray(x, np.float32).astype(ml_dtypes.bfloat16).astype(np.float64), axis, -1)
    blocks = v.reshape(v.shape[:-1] + (-1, 32))
    amax = np.abs(blocks).max(-1, keepdims=True)
    byte = np.maximum(np.where(amax > 0, np.frexp(amax)[1] - 1 + 127, 0) - down, 1)
    scale = np.exp2(byte - 127.0)
    codes = (blocks / scale).astype(np.float32).astype(dtype).astype(np.float64)
    return np.moveaxis((codes * scale).reshape(v.shape), -1, axis)


WIDE = False


def mx_kscale(k):
    if not WIDE:
        return np.ones(k)
    levels = np.array([30, -30])
    if k % 512:
        return np.exp2(np.random.permutation(np.resize(levels, k // 32))).repeat(32)
    a = np.empty((k // 512, 16))
    for p in range(k // 512):
        a[p, :8] = np.random.permutation(np.resize(levels, 8))
        for g in range(8):
            far = levels[np.abs(levels - a[p, g]) >= 10]
            a[p, g + 8] = far[np.random.randint(len(far))]
    return np.exp2(a.ravel()).repeat(32)


def f64(x):
    return np.asarray(x).astype(np.float64)


def striped(idx):
    return np.tile(np.asarray(idx).reshape(-1, 16).T, (8, 1)).astype(np.uint16)


def unstriped(offs):
    return offs[:16].T.reshape(-1).astype(np.int64)


def striped8(idx):
    return np.asarray(idx).reshape(8, -1, 16).transpose(0, 2, 1).reshape(128, -1).astype(np.uint16)


def unstriped8(offs):
    return offs.reshape(8, 16, -1).transpose(0, 2, 1).reshape(8, -1).astype(np.int64)


def pick8(x, idx, run):
    r = np.arange(len(x))
    return x[r[:, None], idx[r % (8 * run) // run]]


E2M1 = np.array([0.0, 0.5, 1.0, 1.5, 2.0, 3.0, 4.0, 6.0, -0.0, -0.5, -1.0, -1.5, -2.0, -3.0, -4.0, -6.0])


def pack_weight(w, fmt):
    k, n = w.shape
    w = f64(np.asarray(w, np.float32).astype(ml_dtypes.bfloat16)).reshape(k // 32, 32, n)
    amax = np.abs(w).max(1)
    if fmt in ("e4m3", "e5m2"):
        byte = np.frexp(amax)[1] - 1 + 127 - (7 if fmt == "e4m3" else 14)
    else:
        mant, ex = np.frexp(amax / 6.0)
        byte = np.where(mant > 0.5, ex, ex - 1) + 127
    byte = np.clip(np.where(amax > 0, byte, 1), 1, 254)
    scaled = (w * np.exp2(127.0 - byte)[:, None, :]).reshape(k, n).astype(np.float32)
    by_word = np.ascontiguousarray(scaled.reshape(k // 512, 128, 4, n).transpose(0, 1, 3, 2))
    if fmt in ("e4m3", "e5m2"):
        words = by_word.astype(ml_dtypes.float8_e4m3fn if fmt == "e4m3" else ml_dtypes.float8_e5m2).view(np.uint8)
    else:
        c = by_word.astype(ml_dtypes.float4_e2m1fn).view(np.uint8) & 0xF
        words = (c[..., 0::2] | (c[..., 1::2] << 4)).reshape(k // 512, 128, 2 * n)
    return np.ascontiguousarray(words), np.ascontiguousarray(byte.astype(np.uint8).reshape(k // 512, 16, n))


def unpack_weight(words, scales, fmt):
    g, _, n = scales.shape
    words = np.ascontiguousarray(words).reshape(g, 128, n, -1)
    if fmt in ("e4m3", "e5m2"):
        vals = words.view(ml_dtypes.float8_e4m3fn if fmt == "e4m3" else ml_dtypes.float8_e5m2).astype(np.float64)
    else:
        nib = np.empty((g, 128, n, 4), np.uint8)
        nib[..., 0::2] = words & 0xF
        nib[..., 1::2] = words >> 4
        vals = E2M1[nib]
    vals = vals * np.repeat(np.exp2(scales.astype(np.float64) - 127.0), 8, axis=1)[..., None]
    return vals.transpose(0, 1, 3, 2).reshape(g * 512, n)


def sgn(shape):
    return np.random.uniform(0.5, 2.0, shape) * np.where(np.random.standard_normal(shape) < 0, -1.0, 1.0)


K, T, J, R, F, Z, C, O, N, S, E = 512, 1024, 256, 512, 512, 1024, 1024, 256, 256, 1024, 512


def setup_inputs():
    n = np.random.standard_normal
    idx = np.random.permutation(T)[:J]
    idx2 = np.random.permutation(Z)[:J]
    idx3 = np.random.permutation(J)[:J]
    idx4 = np.stack([np.random.permutation(C)[:J] for _ in range(8)])
    idx5 = np.stack([np.random.permutation(C)[:O] for _ in range(8)])
    idx6 = np.random.permutation(S)[:N]
    idx7 = np.stack([np.random.permutation(E)[:O] for _ in range(8)])
    fk = mx_kscale(K)
    ff = mx_kscale(F)
    fr = mx_kscale(R)
    xtp = pack_weight(n((K, T)) / fk[:, None], "e4m3")
    xop = pack_weight(n((F, Z)) / ff[:, None], "e2m1")
    wp = pack_weight(n((K, R)) * 1 / np.sqrt(K) * fk[:, None] * fr, "e2m1")
    w0p = pack_weight(n((F, R)) * 1 / np.sqrt(F) * ff[:, None] * fr, "e5m2")
    w2p = pack_weight(n((F, R)) * 1 / np.sqrt(F) * ff[:, None] * fr, "e5m2")
    vsp = pack_weight(n((R, S)) * 1 / np.sqrt(R) / fr[:, None], "e5m2")
    return {
        "xt_words": xtp[0],
        "xt_scales": xtp[1],
        "xo_words": xop[0],
        "xo_scales": xop[1],
        "w_words": wp[0],
        "w_scales": wp[1],
        "w0_words": w0p[0],
        "w0_scales": w0p[1],
        "w2_words": w2p[0],
        "w2_scales": w2p[1],
        "sa": (sgn((R, 1))).astype(np.float32),
        "vs_words": vsp[0],
        "vs_scales": vsp[1],
        "offs": striped(idx),
        "offs2": striped(idx2),
        "offs3": striped(idx3),
        "offs4": striped8(idx4),
        "offs5": striped8(idx5),
        "offs6": striped(idx6),
        "offs7": striped8(idx7),
    }


def reference(xt_words, xt_scales, xo_words, xo_scales, w_words, w_scales, w0_words, w0_scales, w2_words, w2_scales, sa, vs_words, vs_scales, offs, offs2, offs3, offs4, offs5, offs6, offs7):
    idx = unstriped(offs)
    idx2 = unstriped(offs2)
    idx3 = unstriped(offs3)
    idx4 = unstriped8(offs4)
    idx5 = unstriped8(offs5)
    idx6 = unstriped(offs6)
    idx7 = unstriped8(offs7)
    xtu = unpack_weight(xt_words, xt_scales, "e4m3")
    xou = unpack_weight(xo_words, xo_scales, "e2m1")
    wu = unpack_weight(w_words, w_scales, "e2m1")
    w0u = unpack_weight(w0_words, w0_scales, "e5m2")
    w2u = unpack_weight(w2_words, w2_scales, "e5m2")
    vsu = unpack_weight(vs_words, vs_scales, "e5m2")
    xtidxg = xtu[:, idx]
    xoidx2g = xou[:, idx2]
    a = wu.T @ xtidxg + w0u.T @ xoidx2g
    b = w2u.T @ xoidx2g
    h1 = np.maximum(a, b[:, idx3] * f64(sa))
    pw = np.zeros((R, C))
    pw[np.arange(R)[:, None], idx4[np.arange(R) % 512 // 64]] = h1
    hid = pick8(pw, idx5, 64)
    vsidx6g = vsu[:, idx6]
    hidq = mxq(hid, 0, "e4m3")
    p = vsidx6g.T @ hidq
    y = np.zeros((N, E))
    y[np.arange(N)[:, None], idx7[np.arange(N) % 128 // 16]] = p
    return y

@@ -1,0 +1,233 @@
+from contextlib import ExitStack
+
+import concourse.mybir as mybir
+
+F32 = mybir.dt.float32
+BF16 = mybir.dt.bfloat16
+I32 = mybir.dt.int32
+U32 = mybir.dt.uint32
+U16 = mybir.dt.uint16
+U8 = mybir.dt.uint8
+E4M3 = mybir.dt.float8_e4m3fn_x4
+E5M2 = mybir.dt.float8_e5m2_x4
+E2M1 = mybir.dt.float4_e2m1fn_x4
+COPY = mybir.ActivationFunctionType.Copy
+MAX = mybir.AluOpType.max
+
+FLOPS = 469762048
+
+P = 128
+PACK = 4
+TABLE = 1024
+SLOTS = 256
+HIDDEN = 512
+BOARD = 1024
+PAGE = 512
+HALF = 128
+
+
+def tile_list_ownlater_noted_store_ownpage_kernel(
+    tc, xt_words, xt_scales, xo_words, xo_scales, w_words, w_scales, w0_words, w0_scales, w2_words, w2_scales,
+    sa, vs_words, vs_scales, offs, offs2, offs3, offs4, offs5, offs6, offs7, out,
+):
+    nc = tc.nc
+    with ExitStack() as ctx:
+        lists = ctx.enter_context(tc.tile_pool(name="lists", bufs=1))
+        keep = ctx.enter_context(tc.tile_pool(name="keep", bufs=1))
+        psum = ctx.enter_context(tc.psum_pool(name="psum", bufs=4))
+
+        def sb(name, shape, dtype, tag=None):
+            return keep.tile(shape, dtype, name=name, tag=tag or name, align_bytes=64)
+
+        def load_list(name, src):
+            t = lists.tile([P, 16], U16, name=name)
+            nc.sync.dma_start(t[:], src)
+            return t
+
+        def load_words8(queue, name, src, cols):
+            t = sb(name, [P, cols], U32)
+            queue.dma_start(t[:].bitcast(I32), src[0].rearrange("p n t -> p (n t)").bitcast(I32))
+            return t
+
+        def load_words4(queue, name, src, cols):
+            t = sb(name, [P, cols], U16)
+            queue.dma_start(t[:].bitcast(I32), src[0].bitcast(I32))
+            return t
+
+        def table_plane(name):
+            t = sb(name, [P, TABLE], U8)
+            nc.vector.memset(t[:].bitcast(I32), 0)
+            return t
+
+        def load_table_scales(queue, t, src, r):
+            rows = src[0].rearrange("(q r) c -> r q c", r=4)
+            queue.dma_start(t[r:P:32, :].bitcast(I32), rows[r].bitcast(I32))
+
+        def weight_stage(name, parts):
+            t = sb(name, [P, parts, HIDDEN // 4], I32)
+            nc.vector.memset(t[:, 0:4:2, :] if parts == 4 else t[:], 0)
+            return t
+
+        def load_weight_scales1(queue, t, src):
+            queue.dma_start(t[0:4, :, :], src[0].bitcast(I32).rearrange("(q r) c -> r q c", r=4))
+
+        def load_weight_scales2(queue, t, src, q):
+            rows = src[0].bitcast(I32).rearrange("(h q r) c -> q r h c", h=2, q=2)
+            queue.dma_start(t[32 * q : 32 * q + 4, :, :], rows[q])
+
+        def deal_scales(name, t, parts):
+            if parts == 4:
+                nc.vector.tensor_copy(t[32:36, 0:4:2, :], t[0:4, 1:4:2, :])
+            nc.vector.tensor_copy(t[64:128, 0, :], t[0:64, parts // 2, :])
+            d = sb(name, [P, PACK, P], U8)
+            nc.vector.tensor_copy(
+                d[:].rearrange("p t m -> p m t"), t[:, 0, :].bitcast(U8).rearrange("p (m t) -> p m t", t=PACK)
+            )
+            return d
+
+        def deal_words(copy, name, t, dtype, view):
+            d = sb(name, [P, PACK, P], dtype)
+            copy(d[:].bitcast(view).rearrange("p t m -> p m t"), t[:].bitcast(view).rearrange("p (m t) -> p m t", t=PACK))
+            return d
+
+        def deal(copy, dst, src, lo, hi):
+            copy(dst[:, :, lo:hi, :], src.rearrange("p a (m t) -> p a t m", t=PACK)[:, :, lo:hi, :])
+
+        def gather(name, window, offsets, dtype, tag=None):
+            g = sb(name, [P, SLOTS], dtype, tag)
+            nc.vector.tensor_copy(g[:], window[:].indirect(offsets[:]))
+            return g
+
+        xo_s = table_plane("xo_s")
+        w2_s = weight_stage("w2_s", 2)
+        xt_s = table_plane("xt_s")
+        wa_s = sb("wa_s", [P, 2, 2, HIDDEN // 4], I32)
+        nc.vector.memset(wa_s[:], 0)
+        vs_s = table_plane("vs_s")
+        boards = [sb(f"board{t}", [P, BOARD], F32) for t in range(2)]
+        for board in boards:
+            nc.vector.memset(board[:], 0.0)
+
+        l2 = load_list("l2", offs2)
+        for r in range(4):
+            load_table_scales(nc.scalar, xo_s, xo_scales, r)
+        xo_w = load_words4(nc.sync, "xo_w", xo_words, TABLE)
+        w2_w = load_words8(nc.sync, "w2_w", w2_words, HIDDEN)
+        load_weight_scales2(nc.sync, w2_s, w2_scales, 0)
+        load_weight_scales2(nc.gpsimd, w2_s, w2_scales, 1)
+        sa_t = sb("sa_t", [P, PACK], F32)
+        nc.gpsimd.dma_start(sa_t[:], sa.rearrange("(p t) o -> p (t o)", t=PACK))
+        w0_w = load_words8(nc.sync, "w0_w", w0_words, HIDDEN)
+        l3 = load_list("l3", offs3)
+        xt_w = load_words8(nc.sync, "xt_w", xt_words, TABLE)
+        l1 = load_list("l1", offs)
+        for r in range(4):
+            load_table_scales(nc.sync, xt_s, xt_scales, r)
+        for q in range(2):
+            load_weight_scales2(nc.sync, wa_s[:, :, 0, :], w0_scales, q)
+        w_w = load_words4(nc.sync, "w_w", w_words, HIDDEN)
+        for q in range(2):
+            load_weight_scales2(nc.sync, wa_s[:, :, 1, :], w_scales, q)
+        l4 = load_list("l4", offs4)
+        l6 = load_list("l6", offs6)
+        vs_w = load_words8(nc.sync, "vs_w", vs_words, TABLE)
+        for r in range(4):
+            load_table_scales(nc.sync, vs_s, vs_scales, r)
+        l5 = load_list("l5", offs5)
+        l7 = load_list("l7", offs7)
+
+        xo_gw = gather("xo_gw", xo_w, l2, U16)
+        xo_gs = gather("xo_gs", xo_s, l2, U8)
+        nc.vector.tensor_copy(w2_s[64:128, 0, :], w2_s[0:64, 1, :])
+        w2_sd4 = sb("w2_sd", [P, 1, PACK, P], U8)
+        w2_sd = w2_sd4[:, 0, :, :]
+        w2_wd = deal_words(nc.scalar.copy, "w2_wd", w2_w, U32, U32)
+
+        scaled = []
+        for t in range(PACK):
+            if t < 2:
+                deal(nc.vector.tensor_copy, w2_sd4, w2_s[:, 0:1, :].bitcast(U8), t, 1 if t == 0 else PACK)
+            b_ps = psum.tile([P, SLOTS], F32, name="b_ps", tag="bp")
+            nc.tensor.matmul_mx(
+                out=b_ps[:], lhsT=w2_wd[:, t, :].bitcast(E5M2), lhsT_scale=w2_sd[:, t, :],
+                rhs=xo_gw[:].bitcast(E2M1), rhs_scale=xo_gs[:], start=True, stop=True,
+            )
+            b_sb = sb(f"b_sb{t}", [P, SLOTS], F32)
+            nc.scalar.copy(b_sb[:], b_ps[:])
+            sc = sb(f"scaled{t}", [P, SLOTS], F32)
+            for h in range(2):
+                nc.scalar.activation(
+                    out=sc[:, h * HALF : (h + 1) * HALF], in_=b_sb[:].indirect(l3[:, 8 * h : 8 * h + 8]),
+                    func=COPY, scale=sa_t[:, t : t + 1],
+                )
+            scaled.append(sc)
+
+        w0_wd = deal_words(nc.vector.tensor_copy, "w0_wd", w0_w, U32, I32)
+        xt_gw = gather("xt_gw", xt_w, l1, U32)
+        xt_gs = gather("xt_gs", xt_s, l1, U8)
+        w_wd = deal_words(nc.vector.tensor_copy, "w_wd", w_w, U16, U16)
+        nc.vector.tensor_copy(wa_s[64:128, 0, :, :], wa_s[0:64, 1, :, :])
+        wa_sd = sb("wa_sd", [P, 2, PACK, P], U8)
+
+        kept = []
+        for t in range(PACK):
+            if t < 2:
+                deal(nc.vector.tensor_copy, wa_sd, wa_s[:, 0, :, :].bitcast(U8), t, 1 if t == 0 else PACK)
+            a_ps = psum.tile([P, SLOTS], F32, name="a_ps", tag="a")
+            nc.tensor.matmul_mx(
+                out=a_ps[:], lhsT=w0_wd[:, t, :].bitcast(E5M2), lhsT_scale=wa_sd[:, 0, t, :],
+                rhs=xo_gw[:].bitcast(E2M1), rhs_scale=xo_gs[:], start=True, stop=False,
+            )
+            nc.tensor.matmul_mx(
+                out=a_ps[:], lhsT=w_wd[:, t, :].bitcast(E2M1), lhsT_scale=wa_sd[:, 1, t, :],
+                rhs=xt_gw[:].bitcast(E4M3), rhs_scale=xt_gs[:], start=False, stop=True,
+            )
+            k = sb(f"kept{t}", [P, SLOTS], F32)
+            nc.vector.tensor_tensor(k[:], a_ps[:], scaled[t][:], MAX)
+            kept.append(k)
+
+        vs_gw = gather("vs_gw", vs_w, l6, U32)
+        vs_gs = gather("vs_gs", vs_s, l6, U8)
+
+        found = sb("found", [P, PACK, SLOTS], F32)
+        for t in range(PACK):
+            if t < 2:
+                board = boards[t]
+            else:
+                board = sb(f"board{t}", [P, BOARD], F32, f"scaled{t - 2}")
+                nc.gpsimd.memset(board[:], 0.0)
+            nc.scalar.activation(out=board[:].indirect(l4[:]), in_=kept[t][:], func=COPY)
+            nc.vector.tensor_copy(found[:, t, :], board[:].indirect(l5[:]))
+
+        pages = []
+        for n in range(2):
+            page = sb(f"page{n}", [P, PAGE], F32, f"scaled{n + 2}")
+            nc.gpsimd.memset(page[:], 0.0)
+            pages.append(page)
+
+        products = {}
+        for h in range(2):
+            woven = sb(f"woven{h}", [P, HALF, PACK], BF16)
+            nc.vector.tensor_copy(woven[:], found[:, :, h * HALF : (h + 1) * HALF].rearrange("p t o -> p o t"))
+            hid_w = sb(f"hid_w{h}", [P, HALF], U32)
+            hid_s = sb(f"hid_s{h}", [P, HALF], U8)
+            nc.vector.quantize_mx(
+                out=hid_w[:].bitcast(E4M3), scales=hid_s[:], in_=woven[:].rearrange("p o t -> p (o t)")
+            )
+            for n in range(2):
+                p_ps = psum.tile([P, HALF], F32, name="p_ps", tag="bp")
+                nc.tensor.matmul_mx(
+                    out=p_ps[:], lhsT=vs_gw[:, n * P : (n + 1) * P].bitcast(E5M2),
+                    lhsT_scale=vs_gs[:, n * P : (n + 1) * P],
+                    rhs=hid_w[:].bitcast(E4M3), rhs_scale=hid_s[:], start=True, stop=True,
+                )
+                p_sb = sb(f"p_sb{h}{n}", [P, HALF], F32)
+                nc.vector.tensor_copy(p_sb[:], p_ps[:])
+                products[(h, n)] = p_sb
+
+        for n in range(2):
+            for h in range(2):
+                nc.scalar.activation(
+                    out=pages[n][:].indirect(l7[:, 8 * h : 8 * h + 8]), in_=products[(h, n)][:], func=COPY
+                )
+            nc.sync.dma_start(out[n * P : (n + 1) * P, :], pages[n][:])

@@ -98,50 +98,57 @@ def tile_list_ownlater_noted_store_ownpage_kernel(
             nc.vector.tensor_copy(g[:], window[:].indirect(offsets[:]))
             return g
 
+        boards = {}
         xo_s = table_plane("xo_s")
         w2_s = weight_stage("w2_s", 2)
-        xt_s = table_plane("xt_s")
+        xt_y = sb("xt_y", [P, 2, TABLE // 4], I32)
+        nc.vector.memset(xt_y[0:64, :, :], 0)
+        xt_s = sb("xt_s", [P, TABLE], U8)
         wa_s = sb("wa_s", [P, 2, 2, HIDDEN // 4], I32)
         nc.vector.memset(wa_s[:], 0)
         vs_s = table_plane("vs_s")
-        boards = [sb(f"board{t}", [P, BOARD], F32) for t in range(2)]
-        for board in boards:
-            nc.vector.memset(board[:], 0.0)
+        boards[0] = sb("board0", [P, BOARD], F32)
+        nc.vector.memset(boards[0][:], 0.0)
 
         l2 = load_list("l2", offs2)
-        for r in range(4):
-            load_table_scales(nc.scalar, xo_s, xo_scales, r)
+        load_table_scales(nc.scalar, xo_s, xo_scales, 0)
+        load_table_scales(nc.scalar, xo_s, xo_scales, 1)
+        load_table_scales(nc.scalar, xo_s, xo_scales, 2)
+        load_weight_scales2(nc.sync, w2_s, w2_scales, 0)
+        load_weight_scales2(nc.sync, w2_s, w2_scales, 1)
         xo_w = load_words4(nc.sync, "xo_w", xo_words, TABLE)
         w2_w = load_words8(nc.sync, "w2_w", w2_words, HIDDEN)
-        load_weight_scales2(nc.sync, w2_s, w2_scales, 0)
-        load_weight_scales2(nc.gpsimd, w2_s, w2_scales, 1)
-        sa_t = sb("sa_t", [P, PACK], F32)
-        nc.gpsimd.dma_start(sa_t[:], sa.rearrange("(p t) o -> p (t o)", t=PACK))
+        load_table_scales(nc.sync, xo_s, xo_scales, 3)
         w0_w = load_words8(nc.sync, "w0_w", w0_words, HIDDEN)
+        l1 = load_list("l1", offs)
+        load_weight_scales2(nc.sync, xt_y, xt_scales, 0)
+        load_weight_scales2(nc.sync, xt_y, xt_scales, 1)
         l3 = load_list("l3", offs3)
         xt_w = load_words8(nc.sync, "xt_w", xt_words, TABLE)
-        l1 = load_list("l1", offs)
-        for r in range(4):
-            load_table_scales(nc.sync, xt_s, xt_scales, r)
-        for q in range(2):
-            load_weight_scales2(nc.sync, wa_s[:, :, 0, :], w0_scales, q)
         w_w = load_words4(nc.sync, "w_w", w_words, HIDDEN)
-        for q in range(2):
-            load_weight_scales2(nc.sync, wa_s[:, :, 1, :], w_scales, q)
+        sa_t = sb("sa_t", [P, PACK], F32)
+        nc.sync.dma_start(sa_t[:], sa.rearrange("(p t) o -> p (t o)", t=PACK))
+        load_weight_scales2(nc.sync, wa_s[:, :, 0, :], w0_scales, 0)
+        load_weight_scales2(nc.sync, wa_s[:, :, 0, :], w0_scales, 1)
+        load_weight_scales2(nc.sync, wa_s[:, :, 1, :], w_scales, 0)
+        load_weight_scales2(nc.sync, wa_s[:, :, 1, :], w_scales, 1)
         l4 = load_list("l4", offs4)
+        l5 = load_list("l5", offs5)
         l6 = load_list("l6", offs6)
         vs_w = load_words8(nc.sync, "vs_w", vs_words, TABLE)
-        for r in range(4):
-            load_table_scales(nc.sync, vs_s, vs_scales, r)
-        l5 = load_list("l5", offs5)
+        load_table_scales(nc.sync, vs_s, vs_scales, 0)
+        load_table_scales(nc.sync, vs_s, vs_scales, 1)
+        load_table_scales(nc.sync, vs_s, vs_scales, 2)
+        load_table_scales(nc.sync, vs_s, vs_scales, 3)
         l7 = load_list("l7", offs7)
 
-        xo_gw = gather("xo_gw", xo_w, l2, U16)
-        xo_gs = gather("xo_gs", xo_s, l2, U8)
         nc.vector.tensor_copy(w2_s[64:128, 0, :], w2_s[0:64, 1, :])
         w2_sd4 = sb("w2_sd", [P, 1, PACK, P], U8)
         w2_sd = w2_sd4[:, 0, :, :]
+        xo_gw = gather("xo_gw", xo_w, l2, U16)
+        xo_gs = gather("xo_gs", xo_s, l2, U8)
         w2_wd = deal_words(nc.scalar.copy, "w2_wd", w2_w, U32, U32)
+        w0_wd = deal_words(nc.scalar.copy, "w0_wd", w0_w, U32, U32)
 
         scaled = []
         for t in range(PACK):
@@ -152,22 +159,19 @@ def tile_list_ownlater_noted_store_ownpage_kernel(
                 out=b_ps[:], lhsT=w2_wd[:, t, :].bitcast(E5M2), lhsT_scale=w2_sd[:, t, :],
                 rhs=xo_gw[:].bitcast(E2M1), rhs_scale=xo_gs[:], start=True, stop=True,
             )
-            b_sb = sb(f"b_sb{t}", [P, SLOTS], F32)
-            nc.scalar.copy(b_sb[:], b_ps[:])
+            b_sb = sb(f"b_sb{t}", [P, 2 * SLOTS], F32)
+            (nc.vector.tensor_copy if t < 0 else nc.scalar.copy)(b_sb[:, 0:SLOTS], b_ps[:])
             sc = sb(f"scaled{t}", [P, SLOTS], F32)
-            for h in range(2):
-                nc.scalar.activation(
-                    out=sc[:, h * HALF : (h + 1) * HALF], in_=b_sb[:].indirect(l3[:, 8 * h : 8 * h + 8]),
-                    func=COPY, scale=sa_t[:, t : t + 1],
-                )
+            nc.scalar.activation(out=sc[:], in_=b_sb[:].indirect(l3[:]), func=COPY, scale=sa_t[:, t : t + 1])
             scaled.append(sc)
 
-        w0_wd = deal_words(nc.vector.tensor_copy, "w0_wd", w0_w, U32, I32)
-        xt_gw = gather("xt_gw", xt_w, l1, U32)
+        for h in range(2):
+            nc.vector.tensor_copy(xt_s[64 * h : 64 * h + 64, :].bitcast(I32), xt_y[0:64, h, :])
         xt_gs = gather("xt_gs", xt_s, l1, U8)
-        w_wd = deal_words(nc.vector.tensor_copy, "w_wd", w_w, U16, U16)
+        xt_gw = gather("xt_gw", xt_w, l1, U32)
         nc.vector.tensor_copy(wa_s[64:128, 0, :, :], wa_s[0:64, 1, :, :])
         wa_sd = sb("wa_sd", [P, 2, PACK, P], U8)
+        w_wd = deal_words(nc.vector.tensor_copy, "w_wd", w_w, U16, U16)
 
         kept = []
         for t in range(PACK):
@@ -190,29 +194,32 @@ def tile_list_ownlater_noted_store_ownpage_kernel(
         vs_gs = gather("vs_gs", vs_s, l6, U8)
 
         found = sb("found", [P, PACK, SLOTS], F32)
+        woven = sb("woven", [P, SLOTS, PACK], BF16)
         for t in range(PACK):
-            if t < 2:
+            if t in boards:
                 board = boards[t]
             else:
-                board = sb(f"board{t}", [P, BOARD], F32, f"scaled{t - 2}")
+                board = sb(f"board{t}", [P, BOARD], F32, f"scaled{t - len(boards)}")
                 nc.gpsimd.memset(board[:], 0.0)
             nc.scalar.activation(out=board[:].indirect(l4[:]), in_=kept[t][:], func=COPY)
             nc.vector.tensor_copy(found[:, t, :], board[:].indirect(l5[:]))
+            if t == 1:
+                nc.vector.tensor_copy(woven[:, :, 0:2], found[:, 0:2, :].rearrange("p t o -> p o t"))
 
         pages = []
         for n in range(2):
-            page = sb(f"page{n}", [P, PAGE], F32, f"scaled{n + 2}")
+            page = sb(f"page{n}", [P, PAGE], F32, f"kept{n}")
             nc.gpsimd.memset(page[:], 0.0)
             pages.append(page)
 
         products = {}
         for h in range(2):
-            woven = sb(f"woven{h}", [P, HALF, PACK], BF16)
-            nc.vector.tensor_copy(woven[:], found[:, :, h * HALF : (h + 1) * HALF].rearrange("p t o -> p o t"))
+            cols = slice(h * HALF, (h + 1) * HALF)
+            nc.vector.tensor_copy(woven[:, cols, 2:4], found[:, 2:4, cols].rearrange("p t o -> p o t"))
             hid_w = sb(f"hid_w{h}", [P, HALF], U32)
             hid_s = sb(f"hid_s{h}", [P, HALF], U8)
             nc.vector.quantize_mx(
-                out=hid_w[:].bitcast(E4M3), scales=hid_s[:], in_=woven[:].rearrange("p o t -> p (o t)")
+                out=hid_w[:].bitcast(E4M3), scales=hid_s[:], in_=woven[:, cols, :].rearrange("p o t -> p (o t)")
             )
             for n in range(2):
                 p_ps = psum.tile([P, HALF], F32, name="p_ps", tag="bp")

@@ -109,6 +109,8 @@ def tile_list_ownlater_noted_store_ownpage_kernel(
         vs_s = table_plane("vs_s")
         boards[0] = sb("board0", [P, BOARD], F32)
         nc.vector.memset(boards[0][:], 0.0)
+        boards[1] = sb("board1", [P, BOARD], F32)
+        nc.vector.memset(boards[1][:], 0.0)
 
         l2 = load_list("l2", offs2)
         load_table_scales(nc.scalar, xo_s, xo_scales, 0)
@@ -193,7 +195,7 @@ def tile_list_ownlater_noted_store_ownpage_kernel(
         vs_gw = gather("vs_gw", vs_w, l6, U32)
         vs_gs = gather("vs_gs", vs_s, l6, U8)
 
-        found = sb("found", [P, PACK, SLOTS], F32)
+        found = [sb("found_lo", [P, 2, SLOTS], F32), sb("found_hi", [P, 2, SLOTS], F32, "vs_s")]
         woven = sb("woven", [P, SLOTS, PACK], BF16)
         for t in range(PACK):
             if t in boards:
@@ -202,20 +204,20 @@ def tile_list_ownlater_noted_store_ownpage_kernel(
                 board = sb(f"board{t}", [P, BOARD], F32, f"scaled{t - len(boards)}")
                 nc.gpsimd.memset(board[:], 0.0)
             nc.scalar.activation(out=board[:].indirect(l4[:]), in_=kept[t][:], func=COPY)
-            nc.vector.tensor_copy(found[:, t, :], board[:].indirect(l5[:]))
+            nc.vector.tensor_copy(found[t // 2][:, t % 2, :], board[:].indirect(l5[:]))
             if t == 1:
-                nc.vector.tensor_copy(woven[:, :, 0:2], found[:, 0:2, :].rearrange("p t o -> p o t"))
+                nc.vector.tensor_copy(woven[:, :, 0:2], found[0][:].rearrange("p t o -> p o t"))
 
         pages = []
         for n in range(2):
-            page = sb(f"page{n}", [P, PAGE], F32, f"kept{n}")
+            page = sb(f"page{n}", [P, PAGE], F32, f"scaled{n + 2}")
             nc.gpsimd.memset(page[:], 0.0)
             pages.append(page)
 
         products = {}
         for h in range(2):
             cols = slice(h * HALF, (h + 1) * HALF)
-            nc.vector.tensor_copy(woven[:, cols, 2:4], found[:, 2:4, cols].rearrange("p t o -> p o t"))
+            nc.vector.tensor_copy(woven[:, cols, 2:4], found[1][:, :, cols].rearrange("p t o -> p o t"))
             hid_w = sb(f"hid_w{h}", [P, HALF], U32)
             hid_s = sb(f"hid_s{h}", [P, HALF], U8)
             nc.vector.quantize_mx(

@@ -18,12 +18,15 @@ FLOPS = 469762048
 
 P = 128
 PACK = 4
+QUADRANT = 32
 TABLE = 1024
-SLOTS = 256
+ENTRIES = 256
+GROUP = 16
 HIDDEN = 512
 BOARD = 1024
 PAGE = 512
-HALF = 128
+HALF = ENTRIES // 2
+EARLY_BOARDS = 2
 
 
 def tile_list_ownlater_noted_store_ownpage_kernel(
@@ -34,152 +37,136 @@ def tile_list_ownlater_noted_store_ownpage_kernel(
     with ExitStack() as ctx:
         lists = ctx.enter_context(tc.tile_pool(name="lists", bufs=1))
         keep = ctx.enter_context(tc.tile_pool(name="keep", bufs=1))
-        psum = ctx.enter_context(tc.psum_pool(name="psum", bufs=4))
+        psum = ctx.enter_context(tc.psum_pool(name="psum", bufs=PACK))
 
-        def sb(name, shape, dtype, tag=None):
-            return keep.tile(shape, dtype, name=name, tag=tag or name, align_bytes=64)
+        def sb(name, shape, dtype, after=None):
+            return keep.tile(shape, dtype, name=name, tag=after or name, align_bytes=64)
 
         def load_list(name, src):
-            t = lists.tile([P, 16], U16, name=name)
-            nc.sync.dma_start(t[:], src)
-            return t
+            tile = lists.tile([P, ENTRIES // GROUP], U16, name=name)
+            nc.sync.dma_start(tile[:], src)
+            return tile
 
-        def load_words8(queue, name, src, cols):
-            t = sb(name, [P, cols], U32)
-            queue.dma_start(t[:].bitcast(I32), src[0].rearrange("p n t -> p (n t)").bitcast(I32))
-            return t
+        def load_fp8_words(name, src, columns):
+            tile = sb(name, [P, columns], U32)
+            nc.sync.dma_start(tile[:].bitcast(I32), src[0].rearrange("p n t -> p (n t)").bitcast(I32))
+            return tile
 
-        def load_words4(queue, name, src, cols):
-            t = sb(name, [P, cols], U16)
-            queue.dma_start(t[:].bitcast(I32), src[0].bitcast(I32))
-            return t
+        def load_fp4_words(name, src, columns):
+            tile = sb(name, [P, columns], U16)
+            nc.sync.dma_start(tile[:].bitcast(I32), src[0].bitcast(I32))
+            return tile
 
-        def table_plane(name):
-            t = sb(name, [P, TABLE], U8)
-            nc.vector.memset(t[:].bitcast(I32), 0)
-            return t
+        def zeroed_plane(name):
+            tile = sb(name, [P, TABLE], U8)
+            nc.vector.memset(tile[:].bitcast(I32), 0)
+            return tile
 
-        def load_table_scales(queue, t, src, r):
-            rows = src[0].rearrange("(q r) c -> r q c", r=4)
-            queue.dma_start(t[r:P:32, :].bitcast(I32), rows[r].bitcast(I32))
+        def load_plane_rows(queue, plane, src, i):
+            rows = src[0].rearrange("(q r) c -> r q c", r=PACK)
+            queue.dma_start(plane[i:P:QUADRANT, :].bitcast(I32), rows[i].bitcast(I32))
 
-        def weight_stage(name, parts):
-            t = sb(name, [P, parts, HIDDEN // 4], I32)
-            nc.vector.memset(t[:, 0:4:2, :] if parts == 4 else t[:], 0)
-            return t
-
-        def load_weight_scales1(queue, t, src):
-            queue.dma_start(t[0:4, :, :], src[0].bitcast(I32).rearrange("(q r) c -> r q c", r=4))
-
-        def load_weight_scales2(queue, t, src, q):
+        def load_folded_rows(stage, src):
             rows = src[0].bitcast(I32).rearrange("(h q r) c -> q r h c", h=2, q=2)
-            queue.dma_start(t[32 * q : 32 * q + 4, :, :], rows[q])
+            for q in range(2):
+                nc.sync.dma_start(stage[QUADRANT * q : QUADRANT * q + PACK, :, :], rows[q])
 
-        def deal_scales(name, t, parts):
-            if parts == 4:
-                nc.vector.tensor_copy(t[32:36, 0:4:2, :], t[0:4, 1:4:2, :])
-            nc.vector.tensor_copy(t[64:128, 0, :], t[0:64, parts // 2, :])
-            d = sb(name, [P, PACK, P], U8)
-            nc.vector.tensor_copy(
-                d[:].rearrange("p t m -> p m t"), t[:, 0, :].bitcast(U8).rearrange("p (m t) -> p m t", t=PACK)
+        def deal_words(copy, name, words, dtype, view):
+            dealt = sb(name, [P, PACK, P], dtype)
+            copy(
+                dealt[:].bitcast(view).rearrange("p t m -> p m t"),
+                words[:].bitcast(view).rearrange("p (m t) -> p m t", t=PACK),
             )
-            return d
+            return dealt
 
-        def deal_words(copy, name, t, dtype, view):
-            d = sb(name, [P, PACK, P], dtype)
-            copy(d[:].bitcast(view).rearrange("p t m -> p m t"), t[:].bitcast(view).rearrange("p (m t) -> p m t", t=PACK))
-            return d
+        def deal_scales(dealt, planes, t):
+            if t < 2:
+                part = slice(t, PACK if t else 1)
+                nc.vector.tensor_copy(
+                    dealt[:, :, part, :], planes.rearrange("p a (m t) -> p a t m", t=PACK)[:, :, part, :]
+                )
 
-        def deal(copy, dst, src, lo, hi):
-            copy(dst[:, :, lo:hi, :], src.rearrange("p a (m t) -> p a t m", t=PACK)[:, :, lo:hi, :])
+        def gather(name, window, offsets, dtype):
+            picked = sb(name, [P, ENTRIES], dtype)
+            nc.vector.tensor_copy(picked[:], window[:].indirect(offsets[:]))
+            return picked
 
-        def gather(name, window, offsets, dtype, tag=None):
-            g = sb(name, [P, SLOTS], dtype, tag)
-            nc.vector.tensor_copy(g[:], window[:].indirect(offsets[:]))
-            return g
+        def zeroed(engine, name, columns, after=None):
+            tile = sb(name, [P, columns], F32, after)
+            engine.memset(tile[:], 0.0)
+            return tile
 
-        boards = {}
-        xo_s = table_plane("xo_s")
-        w2_s = weight_stage("w2_s", 2)
-        xt_y = sb("xt_y", [P, 2, TABLE // 4], I32)
-        nc.vector.memset(xt_y[0:64, :, :], 0)
+        xo_s = zeroed_plane("xo_s")
+        w2_s = sb("w2_s", [P, 2, HIDDEN // 4], I32)
+        nc.vector.memset(w2_s[0:64, :, :], 0)
+        xt_fold = sb("xt_fold", [P, 2, TABLE // 4], I32)
+        nc.vector.memset(xt_fold[0:64, :, :], 0)
         xt_s = sb("xt_s", [P, TABLE], U8)
         wa_s = sb("wa_s", [P, 2, 2, HIDDEN // 4], I32)
-        nc.vector.memset(wa_s[:], 0)
-        vs_s = table_plane("vs_s")
-        boards[0] = sb("board0", [P, BOARD], F32)
-        nc.vector.memset(boards[0][:], 0.0)
-        boards[1] = sb("board1", [P, BOARD], F32)
-        nc.vector.memset(boards[1][:], 0.0)
+        nc.vector.memset(wa_s[0:64, :, :, :], 0)
+        vs_s = zeroed_plane("vs_s")
+        boards = [zeroed(nc.vector, "board0", BOARD)]
 
-        l2 = load_list("l2", offs2)
-        load_table_scales(nc.scalar, xo_s, xo_scales, 0)
-        load_table_scales(nc.scalar, xo_s, xo_scales, 1)
-        load_table_scales(nc.scalar, xo_s, xo_scales, 2)
-        load_weight_scales2(nc.sync, w2_s, w2_scales, 0)
-        load_weight_scales2(nc.sync, w2_s, w2_scales, 1)
-        xo_w = load_words4(nc.sync, "xo_w", xo_words, TABLE)
-        w2_w = load_words8(nc.sync, "w2_w", w2_words, HIDDEN)
-        load_table_scales(nc.sync, xo_s, xo_scales, 3)
-        w0_w = load_words8(nc.sync, "w0_w", w0_words, HIDDEN)
-        l1 = load_list("l1", offs)
-        load_weight_scales2(nc.sync, xt_y, xt_scales, 0)
-        load_weight_scales2(nc.sync, xt_y, xt_scales, 1)
-        l3 = load_list("l3", offs3)
-        xt_w = load_words8(nc.sync, "xt_w", xt_words, TABLE)
-        w_w = load_words4(nc.sync, "w_w", w_words, HIDDEN)
+        list_notes = load_list("list_notes", offs2)
+        for i in range(PACK - 1):
+            load_plane_rows(nc.scalar, xo_s, xo_scales, i)
+        load_folded_rows(w2_s, w2_scales)
+        xo_w = load_fp4_words("xo_w", xo_words, TABLE)
+        w2_w = load_fp8_words("w2_w", w2_words, HIDDEN)
+        load_plane_rows(nc.sync, xo_s, xo_scales, PACK - 1)
+        w0_w = load_fp8_words("w0_w", w0_words, HIDDEN)
+        list_tokens = load_list("list_tokens", offs)
+        load_folded_rows(xt_fold, xt_scales)
+        list_partners = load_list("list_partners", offs3)
+        xt_w = load_fp8_words("xt_w", xt_words, TABLE)
+        w_w = load_fp4_words("w_w", w_words, HIDDEN)
         sa_t = sb("sa_t", [P, PACK], F32)
         nc.sync.dma_start(sa_t[:], sa.rearrange("(p t) o -> p (t o)", t=PACK))
-        load_weight_scales2(nc.sync, wa_s[:, :, 0, :], w0_scales, 0)
-        load_weight_scales2(nc.sync, wa_s[:, :, 0, :], w0_scales, 1)
-        load_weight_scales2(nc.sync, wa_s[:, :, 1, :], w_scales, 0)
-        load_weight_scales2(nc.sync, wa_s[:, :, 1, :], w_scales, 1)
-        l4 = load_list("l4", offs4)
-        l5 = load_list("l5", offs5)
-        l6 = load_list("l6", offs6)
-        vs_w = load_words8(nc.sync, "vs_w", vs_words, TABLE)
-        load_table_scales(nc.sync, vs_s, vs_scales, 0)
-        load_table_scales(nc.sync, vs_s, vs_scales, 1)
-        load_table_scales(nc.sync, vs_s, vs_scales, 2)
-        load_table_scales(nc.sync, vs_s, vs_scales, 3)
-        l7 = load_list("l7", offs7)
+        load_folded_rows(wa_s[:, :, 0, :], w0_scales)
+        load_folded_rows(wa_s[:, :, 1, :], w_scales)
+        list_put = load_list("list_put", offs4)
+        list_read = load_list("list_read", offs5)
+        list_store = load_list("list_store", offs6)
+        vs_w = load_fp8_words("vs_w", vs_words, TABLE)
+        for i in range(PACK):
+            load_plane_rows(nc.sync, vs_s, vs_scales, i)
+        list_page = load_list("list_page", offs7)
 
         nc.vector.tensor_copy(w2_s[64:128, 0, :], w2_s[0:64, 1, :])
-        w2_sd4 = sb("w2_sd", [P, 1, PACK, P], U8)
-        w2_sd = w2_sd4[:, 0, :, :]
-        xo_gw = gather("xo_gw", xo_w, l2, U16)
-        xo_gs = gather("xo_gs", xo_s, l2, U8)
+        w2_sd = sb("w2_sd", [P, 1, PACK, P], U8)
+        xo_gw = gather("xo_gw", xo_w, list_notes, U16)
+        xo_gs = gather("xo_gs", xo_s, list_notes, U8)
         w2_wd = deal_words(nc.scalar.copy, "w2_wd", w2_w, U32, U32)
         w0_wd = deal_words(nc.scalar.copy, "w0_wd", w0_w, U32, U32)
 
         scaled = []
         for t in range(PACK):
-            if t < 2:
-                deal(nc.vector.tensor_copy, w2_sd4, w2_s[:, 0:1, :].bitcast(U8), t, 1 if t == 0 else PACK)
-            b_ps = psum.tile([P, SLOTS], F32, name="b_ps", tag="bp")
+            deal_scales(w2_sd, w2_s[:, 0:1, :].bitcast(U8), t)
+            b_ps = psum.tile([P, ENTRIES], F32, name="b_ps", tag="bp")
             nc.tensor.matmul_mx(
-                out=b_ps[:], lhsT=w2_wd[:, t, :].bitcast(E5M2), lhsT_scale=w2_sd[:, t, :],
+                out=b_ps[:], lhsT=w2_wd[:, t, :].bitcast(E5M2), lhsT_scale=w2_sd[:, 0, t, :],
                 rhs=xo_gw[:].bitcast(E2M1), rhs_scale=xo_gs[:], start=True, stop=True,
             )
-            b_sb = sb(f"b_sb{t}", [P, 2 * SLOTS], F32)
-            (nc.vector.tensor_copy if t < 0 else nc.scalar.copy)(b_sb[:, 0:SLOTS], b_ps[:])
-            sc = sb(f"scaled{t}", [P, SLOTS], F32)
-            nc.scalar.activation(out=sc[:], in_=b_sb[:].indirect(l3[:]), func=COPY, scale=sa_t[:, t : t + 1])
-            scaled.append(sc)
+            b_sb = sb(f"b_sb{t}", [P, 2 * ENTRIES], F32)
+            nc.scalar.copy(b_sb[:, 0:ENTRIES], b_ps[:])
+            partner = sb(f"scaled{t}", [P, ENTRIES], F32)
+            nc.scalar.activation(
+                out=partner[:], in_=b_sb[:].indirect(list_partners[:]), func=COPY, scale=sa_t[:, t : t + 1]
+            )
+            scaled.append(partner)
 
-        for h in range(2):
-            nc.vector.tensor_copy(xt_s[64 * h : 64 * h + 64, :].bitcast(I32), xt_y[0:64, h, :])
-        xt_gs = gather("xt_gs", xt_s, l1, U8)
-        xt_gw = gather("xt_gw", xt_w, l1, U32)
+        for fold in range(2):
+            nc.vector.tensor_copy(xt_s[64 * fold : 64 * fold + 64, :].bitcast(I32), xt_fold[0:64, fold, :])
+        xt_gs = gather("xt_gs", xt_s, list_tokens, U8)
+        xt_gw = gather("xt_gw", xt_w, list_tokens, U32)
         nc.vector.tensor_copy(wa_s[64:128, 0, :, :], wa_s[0:64, 1, :, :])
         wa_sd = sb("wa_sd", [P, 2, PACK, P], U8)
         w_wd = deal_words(nc.vector.tensor_copy, "w_wd", w_w, U16, U16)
 
         kept = []
         for t in range(PACK):
-            if t < 2:
-                deal(nc.vector.tensor_copy, wa_sd, wa_s[:, 0, :, :].bitcast(U8), t, 1 if t == 0 else PACK)
-            a_ps = psum.tile([P, SLOTS], F32, name="a_ps", tag="a")
+            deal_scales(wa_sd, wa_s[:, 0, :, :].bitcast(U8), t)
+            a_ps = psum.tile([P, ENTRIES], F32, name="a_ps", tag="a")
             nc.tensor.matmul_mx(
                 out=a_ps[:], lhsT=w0_wd[:, t, :].bitcast(E5M2), lhsT_scale=wa_sd[:, 0, t, :],
                 rhs=xo_gw[:].bitcast(E2M1), rhs_scale=xo_gs[:], start=True, stop=False,
@@ -188,55 +175,50 @@ def tile_list_ownlater_noted_store_ownpage_kernel(
                 out=a_ps[:], lhsT=w_wd[:, t, :].bitcast(E2M1), lhsT_scale=wa_sd[:, 1, t, :],
                 rhs=xt_gw[:].bitcast(E4M3), rhs_scale=xt_gs[:], start=False, stop=True,
             )
-            k = sb(f"kept{t}", [P, SLOTS], F32)
-            nc.vector.tensor_tensor(k[:], a_ps[:], scaled[t][:], MAX)
-            kept.append(k)
+            if t == EARLY_BOARDS - 1:
+                boards.append(zeroed(nc.vector, f"board{t}", BOARD, after="wa_s"))
+            larger = sb(f"kept{t}", [P, ENTRIES], F32)
+            nc.vector.tensor_tensor(larger[:], a_ps[:], scaled[t][:], MAX)
+            kept.append(larger)
 
-        vs_gw = gather("vs_gw", vs_w, l6, U32)
-        vs_gs = gather("vs_gs", vs_s, l6, U8)
+        vs_gw = gather("vs_gw", vs_w, list_store, U32)
+        vs_gs = gather("vs_gs", vs_s, list_store, U8)
 
-        found = [sb("found_lo", [P, 2, SLOTS], F32), sb("found_hi", [P, 2, SLOTS], F32, "vs_s")]
-        woven = sb("woven", [P, SLOTS, PACK], BF16)
+        found = [sb("found_lo", [P, 2, ENTRIES], F32), sb("found_hi", [P, 2, ENTRIES], F32, after="vs_s")]
+        woven = sb("woven", [P, ENTRIES, PACK], BF16)
         for t in range(PACK):
-            if t in boards:
-                board = boards[t]
-            else:
-                board = sb(f"board{t}", [P, BOARD], F32, f"scaled{t - len(boards)}")
-                nc.gpsimd.memset(board[:], 0.0)
-            nc.scalar.activation(out=board[:].indirect(l4[:]), in_=kept[t][:], func=COPY)
-            nc.vector.tensor_copy(found[t // 2][:, t % 2, :], board[:].indirect(l5[:]))
+            if t >= EARLY_BOARDS:
+                boards.append(zeroed(nc.gpsimd, f"board{t}", BOARD, after=f"scaled{t - EARLY_BOARDS}"))
+            nc.scalar.activation(out=boards[t][:].indirect(list_put[:]), in_=kept[t][:], func=COPY)
+            nc.vector.tensor_copy(found[t // 2][:, t % 2, :], boards[t][:].indirect(list_read[:]))
             if t == 1:
                 nc.vector.tensor_copy(woven[:, :, 0:2], found[0][:].rearrange("p t o -> p o t"))
 
-        pages = []
-        for n in range(2):
-            page = sb(f"page{n}", [P, PAGE], F32, f"scaled{n + 2}")
-            nc.gpsimd.memset(page[:], 0.0)
-            pages.append(page)
+        pages = [zeroed(nc.gpsimd, f"page{u}", PAGE, after=f"scaled{u + EARLY_BOARDS}") for u in range(2)]
 
         products = {}
         for h in range(2):
-            cols = slice(h * HALF, (h + 1) * HALF)
-            nc.vector.tensor_copy(woven[:, cols, 2:4], found[1][:, :, cols].rearrange("p t o -> p o t"))
+            places = slice(h * HALF, (h + 1) * HALF)
+            nc.vector.tensor_copy(woven[:, places, 2:4], found[1][:, :, places].rearrange("p t o -> p o t"))
             hid_w = sb(f"hid_w{h}", [P, HALF], U32)
             hid_s = sb(f"hid_s{h}", [P, HALF], U8)
             nc.vector.quantize_mx(
-                out=hid_w[:].bitcast(E4M3), scales=hid_s[:], in_=woven[:, cols, :].rearrange("p o t -> p (o t)")
+                out=hid_w[:].bitcast(E4M3), scales=hid_s[:], in_=woven[:, places, :].rearrange("p o t -> p (o t)")
             )
-            for n in range(2):
+            for u in range(2):
+                features = slice(u * P, (u + 1) * P)
                 p_ps = psum.tile([P, HALF], F32, name="p_ps", tag="bp")
                 nc.tensor.matmul_mx(
-                    out=p_ps[:], lhsT=vs_gw[:, n * P : (n + 1) * P].bitcast(E5M2),
-                    lhsT_scale=vs_gs[:, n * P : (n + 1) * P],
+                    out=p_ps[:], lhsT=vs_gw[:, features].bitcast(E5M2), lhsT_scale=vs_gs[:, features],
                     rhs=hid_w[:].bitcast(E4M3), rhs_scale=hid_s[:], start=True, stop=True,
                 )
-                p_sb = sb(f"p_sb{h}{n}", [P, HALF], F32)
+                p_sb = sb(f"p_sb{h}{u}", [P, HALF], F32)
                 nc.vector.tensor_copy(p_sb[:], p_ps[:])
-                products[(h, n)] = p_sb
+                products[(h, u)] = p_sb
 
-        for n in range(2):
+        half_columns = HALF // GROUP
+        for u in range(2):
             for h in range(2):
-                nc.scalar.activation(
-                    out=pages[n][:].indirect(l7[:, 8 * h : 8 * h + 8]), in_=products[(h, n)][:], func=COPY
-                )
-            nc.sync.dma_start(out[n * P : (n + 1) * P, :], pages[n][:])
+                offsets = list_page[:, h * half_columns : (h + 1) * half_columns]
+                nc.scalar.activation(out=pages[u][:].indirect(offsets), in_=products[(h, u)][:], func=COPY)
+            nc.sync.dma_start(out[u * P : (u + 1) * P, :], pages[u][:])

from contextlib import ExitStack

import concourse.mybir as mybir

F32 = mybir.dt.float32
BF16 = mybir.dt.bfloat16
I32 = mybir.dt.int32
U32 = mybir.dt.uint32
U16 = mybir.dt.uint16
U8 = mybir.dt.uint8
E4M3 = mybir.dt.float8_e4m3fn_x4
E5M2 = mybir.dt.float8_e5m2_x4
E2M1 = mybir.dt.float4_e2m1fn_x4
COPY = mybir.ActivationFunctionType.Copy
MAX = mybir.AluOpType.max

FLOPS = 469762048

P = 128
PACK = 4
QUADRANT = 32
TABLE = 1024
ENTRIES = 256
GROUP = 16
HIDDEN = 512
BOARD = 1024
PAGE = 512
HALF = ENTRIES // 2
EARLY_BOARDS = 2


def tile_list_ownlater_noted_store_ownpage_kernel(
    tc, xt_words, xt_scales, xo_words, xo_scales, w_words, w_scales, w0_words, w0_scales, w2_words, w2_scales,
    sa, vs_words, vs_scales, offs, offs2, offs3, offs4, offs5, offs6, offs7, out,
):
    nc = tc.nc
    with ExitStack() as ctx:
        lists = ctx.enter_context(tc.tile_pool(name="lists", bufs=1))
        keep = ctx.enter_context(tc.tile_pool(name="keep", bufs=1))
        psum = ctx.enter_context(tc.psum_pool(name="psum", bufs=PACK))

        def sb(name, shape, dtype, after=None):
            return keep.tile(shape, dtype, name=name, tag=after or name, align_bytes=64)

        def load_list(name, src):
            tile = lists.tile([P, ENTRIES // GROUP], U16, name=name)
            nc.sync.dma_start(tile[:], src)
            return tile

        def load_fp8_words(name, src, columns):
            tile = sb(name, [P, columns], U32)
            nc.sync.dma_start(tile[:].bitcast(I32), src[0].rearrange("p n t -> p (n t)").bitcast(I32))
            return tile

        def load_fp4_words(name, src, columns):
            tile = sb(name, [P, columns], U16)
            nc.sync.dma_start(tile[:].bitcast(I32), src[0].bitcast(I32))
            return tile

        def zeroed_plane(name):
            tile = sb(name, [P, TABLE], U8)
            nc.vector.memset(tile[:].bitcast(I32), 0)
            return tile

        def load_plane_rows(queue, plane, src, i):
            rows = src[0].rearrange("(q r) c -> r q c", r=PACK)
            queue.dma_start(plane[i:P:QUADRANT, :].bitcast(I32), rows[i].bitcast(I32))

        def load_folded_rows(stage, src):
            rows = src[0].bitcast(I32).rearrange("(h q r) c -> q r h c", h=2, q=2)
            for q in range(2):
                nc.sync.dma_start(stage[QUADRANT * q : QUADRANT * q + PACK, :, :], rows[q])

        def deal_words(copy, name, words, dtype, view):
            dealt = sb(name, [P, PACK, P], dtype)
            copy(
                dealt[:].bitcast(view).rearrange("p t m -> p m t"),
                words[:].bitcast(view).rearrange("p (m t) -> p m t", t=PACK),
            )
            return dealt

        def deal_scales(dealt, planes, t):
            if t < 2:
                part = slice(t, PACK if t else 1)
                nc.vector.tensor_copy(
                    dealt[:, :, part, :], planes.rearrange("p a (m t) -> p a t m", t=PACK)[:, :, part, :]
                )

        def gather(name, window, offsets, dtype):
            picked = sb(name, [P, ENTRIES], dtype)
            nc.vector.tensor_copy(picked[:], window[:].indirect(offsets[:]))
            return picked

        def zeroed(engine, name, columns, after=None):
            tile = sb(name, [P, columns], F32, after)
            engine.memset(tile[:], 0.0)
            return tile

        xo_s = zeroed_plane("xo_s")
        w2_s = sb("w2_s", [P, 2, HIDDEN // 4], I32)
        nc.vector.memset(w2_s[0:64, :, :], 0)
        xt_fold = sb("xt_fold", [P, 2, TABLE // 4], I32)
        nc.vector.memset(xt_fold[0:64, :, :], 0)
        xt_s = sb("xt_s", [P, TABLE], U8)
        wa_s = sb("wa_s", [P, 2, 2, HIDDEN // 4], I32)
        nc.vector.memset(wa_s[0:64, :, :, :], 0)
        vs_s = zeroed_plane("vs_s")
        boards = [zeroed(nc.vector, "board0", BOARD)]

        list_notes = load_list("list_notes", offs2)
        for i in range(PACK - 1):
            load_plane_rows(nc.scalar, xo_s, xo_scales, i)
        load_folded_rows(w2_s, w2_scales)
        xo_w = load_fp4_words("xo_w", xo_words, TABLE)
        w2_w = load_fp8_words("w2_w", w2_words, HIDDEN)
        load_plane_rows(nc.sync, xo_s, xo_scales, PACK - 1)
        w0_w = load_fp8_words("w0_w", w0_words, HIDDEN)
        list_tokens = load_list("list_tokens", offs)
        load_folded_rows(xt_fold, xt_scales)
        list_partners = load_list("list_partners", offs3)
        xt_w = load_fp8_words("xt_w", xt_words, TABLE)
        w_w = load_fp4_words("w_w", w_words, HIDDEN)
        sa_t = sb("sa_t", [P, PACK], F32)
        nc.sync.dma_start(sa_t[:], sa.rearrange("(p t) o -> p (t o)", t=PACK))
        load_folded_rows(wa_s[:, :, 0, :], w0_scales)
        load_folded_rows(wa_s[:, :, 1, :], w_scales)
        list_put = load_list("list_put", offs4)
        list_read = load_list("list_read", offs5)
        list_store = load_list("list_store", offs6)
        vs_w = load_fp8_words("vs_w", vs_words, TABLE)
        for i in range(PACK):
            load_plane_rows(nc.sync, vs_s, vs_scales, i)
        list_page = load_list("list_page", offs7)

        nc.vector.tensor_copy(w2_s[64:128, 0, :], w2_s[0:64, 1, :])
        w2_sd = sb("w2_sd", [P, 1, PACK, P], U8)
        xo_gw = gather("xo_gw", xo_w, list_notes, U16)
        xo_gs = gather("xo_gs", xo_s, list_notes, U8)
        w2_wd = deal_words(nc.scalar.copy, "w2_wd", w2_w, U32, U32)
        w0_wd = deal_words(nc.scalar.copy, "w0_wd", w0_w, U32, U32)

        scaled = []
        for t in range(PACK):
            deal_scales(w2_sd, w2_s[:, 0:1, :].bitcast(U8), t)
            b_ps = psum.tile([P, ENTRIES], F32, name="b_ps", tag="bp")
            nc.tensor.matmul_mx(
                out=b_ps[:], lhsT=w2_wd[:, t, :].bitcast(E5M2), lhsT_scale=w2_sd[:, 0, t, :],
                rhs=xo_gw[:].bitcast(E2M1), rhs_scale=xo_gs[:], start=True, stop=True,
            )
            b_sb = sb(f"b_sb{t}", [P, 2 * ENTRIES], F32)
            nc.scalar.copy(b_sb[:, 0:ENTRIES], b_ps[:])
            partner = sb(f"scaled{t}", [P, ENTRIES], F32)
            nc.scalar.activation(
                out=partner[:], in_=b_sb[:].indirect(list_partners[:]), func=COPY, scale=sa_t[:, t : t + 1]
            )
            scaled.append(partner)

        for fold in range(2):
            nc.vector.tensor_copy(xt_s[64 * fold : 64 * fold + 64, :].bitcast(I32), xt_fold[0:64, fold, :])
        xt_gs = gather("xt_gs", xt_s, list_tokens, U8)
        xt_gw = gather("xt_gw", xt_w, list_tokens, U32)
        nc.vector.tensor_copy(wa_s[64:128, 0, :, :], wa_s[0:64, 1, :, :])
        wa_sd = sb("wa_sd", [P, 2, PACK, P], U8)
        w_wd = deal_words(nc.vector.tensor_copy, "w_wd", w_w, U16, U16)

        kept = []
        for t in range(PACK):
            deal_scales(wa_sd, wa_s[:, 0, :, :].bitcast(U8), t)
            a_ps = psum.tile([P, ENTRIES], F32, name="a_ps", tag="a")
            nc.tensor.matmul_mx(
                out=a_ps[:], lhsT=w0_wd[:, t, :].bitcast(E5M2), lhsT_scale=wa_sd[:, 0, t, :],
                rhs=xo_gw[:].bitcast(E2M1), rhs_scale=xo_gs[:], start=True, stop=False,
            )
            nc.tensor.matmul_mx(
                out=a_ps[:], lhsT=w_wd[:, t, :].bitcast(E2M1), lhsT_scale=wa_sd[:, 1, t, :],
                rhs=xt_gw[:].bitcast(E4M3), rhs_scale=xt_gs[:], start=False, stop=True,
            )
            if t == EARLY_BOARDS - 1:
                boards.append(zeroed(nc.vector, f"board{t}", BOARD, after="wa_s"))
            larger = sb(f"kept{t}", [P, ENTRIES], F32)
            nc.vector.tensor_tensor(larger[:], a_ps[:], scaled[t][:], MAX)
            kept.append(larger)

        vs_gw = gather("vs_gw", vs_w, list_store, U32)
        vs_gs = gather("vs_gs", vs_s, list_store, U8)

        found = [sb("found_lo", [P, 2, ENTRIES], F32), sb("found_hi", [P, 2, ENTRIES], F32, after="vs_s")]
        woven = sb("woven", [P, ENTRIES, PACK], BF16)
        for t in range(PACK):
            if t >= EARLY_BOARDS:
                boards.append(zeroed(nc.gpsimd, f"board{t}", BOARD, after=f"scaled{t - EARLY_BOARDS}"))
            nc.scalar.activation(out=boards[t][:].indirect(list_put[:]), in_=kept[t][:], func=COPY)
            nc.vector.tensor_copy(found[t // 2][:, t % 2, :], boards[t][:].indirect(list_read[:]))
            if t == 1:
                nc.vector.tensor_copy(woven[:, :, 0:2], found[0][:].rearrange("p t o -> p o t"))

        pages = [zeroed(nc.gpsimd, f"page{u}", PAGE, after=f"scaled{u + EARLY_BOARDS}") for u in range(2)]

        products = {}
        for h in range(2):
            places = slice(h * HALF, (h + 1) * HALF)
            nc.vector.tensor_copy(woven[:, places, 2:4], found[1][:, :, places].rearrange("p t o -> p o t"))
            hid_w = sb(f"hid_w{h}", [P, HALF], U32)
            hid_s = sb(f"hid_s{h}", [P, HALF], U8)
            nc.vector.quantize_mx(
                out=hid_w[:].bitcast(E4M3), scales=hid_s[:], in_=woven[:, places, :].rearrange("p o t -> p (o t)")
            )
            for u in range(2):
                features = slice(u * P, (u + 1) * P)
                p_ps = psum.tile([P, HALF], F32, name="p_ps", tag="bp")
                nc.tensor.matmul_mx(
                    out=p_ps[:], lhsT=vs_gw[:, features].bitcast(E5M2), lhsT_scale=vs_gs[:, features],
                    rhs=hid_w[:].bitcast(E4M3), rhs_scale=hid_s[:], start=True, stop=True,
                )
                p_sb = sb(f"p_sb{h}{u}", [P, HALF], F32)
                nc.vector.tensor_copy(p_sb[:], p_ps[:])
                products[(h, u)] = p_sb

        half_columns = HALF // GROUP
        for u in range(2):
            for h in range(2):
                offsets = list_page[:, h * half_columns : (h + 1) * half_columns]
                nc.scalar.activation(out=pages[u][:].indirect(offsets), in_=products[(h, u)][:], func=COPY)
            nc.sync.dma_start(out[u * P : (u + 1) * P, :], pages[u][:])
